import numpy as np
import ml_dtypes


def mxq(x, axis, fmt="e4m3"):
    dtype, down = {"e4m3": (ml_dtypes.float8_e4m3fn, 7), "e5m2": (ml_dtypes.float8_e5m2, 14)}[fmt]
    v = np.moveaxis(np.asarray(x, np.float32).astype(ml_dtypes.bfloat16).astype(np.float64), axis, -1)
    blocks = v.reshape(v.shape[:-1] + (-1, 32))
    amax = np.abs(blocks).max(-1, keepdims=True)
    byte = np.maximum(np.where(amax > 0, np.frexp(amax)[1] - 1 + 127, 0) - down, 1)
    scale = np.exp2(byte - 127.0)
    codes = (blocks / scale).astype(np.float32).astype(dtype).astype(np.float64)
    return np.moveaxis((codes * scale).reshape(v.shape), -1, axis)


WIDE = False


def mx_kscale(k):
    if not WIDE:
        return np.ones(k)
    levels = np.array([10, -10, 5, -5, 0])
    if k % 512:
        return np.exp2(np.random.permutation(np.resize(levels, k // 32))).repeat(32)
    a = np.empty((k // 512, 16))
    for p in range(k // 512):
        a[p, :8] = np.random.permutation(np.resize(levels, 8))
        for g in range(8):
            far = levels[np.abs(levels - a[p, g]) >= 10]
            a[p, g + 8] = far[np.random.randint(len(far))]
    return np.exp2(a.ravel()).repeat(32)


def f64(x):
    return np.asarray(x).astype(np.float64)


def striped8(idx):
    return np.asarray(idx).reshape(8, -1, 16).transpose(0, 2, 1).reshape(128, -1).astype(np.uint16)


def unstriped8(offs):
    return offs.reshape(8, 16, -1).transpose(0, 2, 1).reshape(8, -1).astype(np.int64)


def pick8(x, idx, run):
    r = np.arange(len(x))
    return x[r[:, None], idx[r % (8 * run) // run]]


E2M1 = np.array([0.0, 0.5, 1.0, 1.5, 2.0, 3.0, 4.0, 6.0, -0.0, -0.5, -1.0, -1.5, -2.0, -3.0, -4.0, -6.0])


def pack_weight(w, fmt):
    k, n = w.shape
    w = f64(np.asarray(w, np.float32).astype(ml_dtypes.bfloat16)).reshape(k // 32, 32, n)
    amax = np.abs(w).max(1)
    if fmt == "e4m3":
        byte = np.frexp(amax)[1] - 1 + 127 - 7
    else:
        mant, ex = np.frexp(amax / 6.0)
        byte = np.where(mant > 0.5, ex, ex - 1) + 127
    byte = np.clip(np.where(amax > 0, byte, 1), 1, 254)
    scaled = (w * np.exp2(127.0 - byte)[:, None, :]).reshape(k, n).astype(np.float32)
    by_word = np.ascontiguousarray(scaled.reshape(k // 512, 128, 4, n).transpose(0, 1, 3, 2))
    if fmt == "e4m3":
        words = by_word.astype(ml_dtypes.float8_e4m3fn).view(np.uint8)
    else:
        c = by_word.astype(ml_dtypes.float4_e2m1fn).view(np.uint8) & 0xF
        words = (c[..., 0::2] | (c[..., 1::2] << 4)).reshape(k // 512, 128, 2 * n)
    return np.ascontiguousarray(words), np.ascontiguousarray(byte.astype(np.uint8).reshape(k // 512, 16, n))


def unpack_weight(words, scales, fmt):
    g, _, n = scales.shape
    words = np.ascontiguousarray(words).reshape(g, 128, n, -1)
    if fmt == "e4m3":
        vals = words.view(ml_dtypes.float8_e4m3fn).astype(np.float64)
    else:
        nib = np.empty((g, 128, n, 4), np.uint8)
        nib[..., 0::2] = words & 0xF
        nib[..., 1::2] = words >> 4
        vals = E2M1[nib]
    vals = vals * np.repeat(np.exp2(scales.astype(np.float64) - 127.0), 8, axis=1)[..., None]
    return vals.transpose(0, 1, 3, 2).reshape(g * 512, n)


D, V, Q, I = 512, 2048, 128, 1024


def setup_inputs():
    n = np.random.standard_normal
    idx = np.stack([np.random.permutation(V)[:I] for _ in range(8)])
    fd = mx_kscale(D)
    vocp = pack_weight(n((D, V)) / fd[:, None], "e4m3")
    return {
        "hid": (n((D, Q)) * 1.0 / np.sqrt(D) * fd[:, None]).astype(np.float32),
        "voc_words": vocp[0],
        "voc_scales": vocp[1],
        "fine": (np.random.uniform(8.0, 12.0, (Q, 1))).astype(np.float32),
        "offs": striped8(idx),
    }


def reference(hid, voc_words, voc_scales, fine, offs):
    idx = unstriped8(offs)
    vocu = unpack_weight(voc_words, voc_scales, "e4m3")
    hidq = mxq(f64(hid), 0, "e4m3")
    a = hidq.T @ vocu
    m1 = np.max(pick8(a, idx, 16), axis=1, keepdims=True)
    r = np.exp(pick8(a, idx, 16) - m1)
    up = f64(fine) - m1 - np.log(np.sum(r, axis=1, keepdims=True))
    dl = pick8(a, idx, 16) + up
    df = np.zeros((Q, V))
    df[np.arange(Q)[:, None], idx[np.arange(Q) % 128 // 16]] = dl
    y = df - f64(fine)
    return y

@@ -1,0 +1,144 @@
+from contextlib import ExitStack
+
+import concourse.mybir as mybir
+
+D, V, Q, I = 512, 2048, 128, 1024
+FLOPS = 2 * D * V * Q
+
+F32 = mybir.dt.float32
+BF16 = mybir.dt.bfloat16
+I32 = mybir.dt.int32
+U32 = mybir.dt.uint32
+U16 = mybir.dt.uint16
+U8 = mybir.dt.uint8
+FP8X4 = mybir.dt.float8_e4m3fn_x4
+ALU = mybir.AluOpType
+ACT = mybir.ActivationFunctionType
+AX = mybir.AxisListType
+
+P = 128
+PACK = 4
+PLANE = 512
+HALF = I // 2
+WORD_LOADS = ((0, 1024), (1024, 1536), (1536, 2048))
+PRODUCTS = ((0, 512), (512, 1024), (1024, 1536), (1536, 1792), (1792, 2048))
+FIRST = 256
+VECTOR_STORES = ((0, 256), (256, 768), (768, 1536))
+SCALAR_STORE = (1536, 2048)
+
+
+def tile_attend_allowedset_heads_kernel(tc, hid, voc_words, voc_scales, fine, offs, out):
+    nc = tc.nc
+    with ExitStack() as ctx:
+        pool = ctx.enter_context(tc.tile_pool(name="pool", bufs=1))
+        psum = ctx.enter_context(tc.psum_pool(name="psum", bufs=1))
+
+        offsets = pool.tile([P, I // 16], U16, name="offsets")
+        planes = pool.tile([P, PLANE], U8, name="planes", align_bytes=64)
+        nc.vector.memset(planes[:].bitcast(I32), 0)
+        for quad in range(4):
+            rows = voc_scales[0][4 * quad : 4 * quad + 4, :].bitcast(I32)
+            nc.scalar.dma_start(
+                out=planes[32 * quad : 32 * quad + 16, :].bitcast(I32),
+                in_=rows.rearrange("r (c w) -> c r w", c=4),
+            )
+
+        hid_raw = pool.tile([P, PACK, Q], F32, name="hid_raw")
+        nc.sync.dma_start(out=hid_raw[:], in_=hid.rearrange("(p j) q -> p j q", j=PACK))
+        all_words = voc_words[0].rearrange("p n t -> p (n t)").bitcast(I32)
+        words = []
+        for n, (lo, hi) in enumerate(WORD_LOADS):
+            part = pool.tile([P, hi - lo], U32, name="words%d" % n, align_bytes=64)
+            nc.sync.dma_start(out=part[:].bitcast(I32), in_=all_words[:, lo:hi])
+            words.append(part)
+        nc.sync.dma_start(offsets[:], offs)
+        fine_col = pool.tile([P, 1], F32, name="fine_col")
+        nc.sync.dma_start(out=fine_col[:], in_=fine)
+
+        placed = pool.tile([P, V], F32, name="placed")
+        nc.vector.memset(placed[:], 0.0)
+
+        hid_bf = pool.tile([P, Q, PACK], BF16, name="hid_bf", align_bytes=64)
+        nc.vector.tensor_copy(
+            out=hid_bf[:].rearrange("p (c i) t -> p c t i", i=4),
+            in_=hid_raw[:].rearrange("p t (c i) -> p c t i", i=4),
+        )
+        hid_codes = pool.tile([P, Q], U32, name="hid_codes", align_bytes=64)
+        hid_scales = pool.tile([P, Q], U8, name="hid_scales", align_bytes=64)
+        nc.vector.quantize_mx(
+            out=hid_codes[:].bitcast(FP8X4),
+            scales=hid_scales[:],
+            in_=hid_bf[:].rearrange("p q t -> p (q t)"),
+        )
+
+        scores = pool.tile([P, V], F32, name="scores")
+        for n, (lo, hi) in enumerate(PRODUCTS):
+            load = max(k for k, (start, end) in enumerate(WORD_LOADS) if start <= lo)
+            base = WORD_LOADS[load][0]
+            c = lo // PLANE
+            bank = psum.tile([P, hi - lo], F32, name="bank%d" % n)
+            nc.tensor.matmul_mx(
+                out=bank[:],
+                lhsT=hid_codes[:].bitcast(FP8X4),
+                lhsT_scale=hid_scales[:],
+                rhs=words[load][:, lo - base : hi - base].bitcast(FP8X4),
+                rhs_scale=planes[4 * c : P, lo - c * PLANE : hi - c * PLANE],
+                start=True,
+                stop=True,
+            )
+            if n % 2 == 0:
+                nc.scalar.copy(out=scores[:, lo:hi], in_=bank[:])
+            else:
+                nc.vector.tensor_copy(out=scores[:, lo:hi], in_=bank[:])
+
+        picked = pool.tile([P, I], F32, name="picked")
+        for h in range(2):
+            nc.vector.tensor_copy(
+                out=picked[:, h * HALF : (h + 1) * HALF],
+                in_=scores[:].indirect(offsets[:, h * HALF // 16 : (h + 1) * HALF // 16]),
+            )
+        neg_max = pool.tile([P, 2], F32, name="neg_max")
+        sums = pool.tile([P, 2], F32, name="sums")
+        exps = pool.tile([P, I], BF16, name="exps")
+        for h in range(2):
+            cols = slice(h * HALF, (h + 1) * HALF)
+            nc.vector.tensor_reduce(out=neg_max[:, h : h + 1], in_=picked[:, cols], axis=AX.X, op=ALU.max, negate=True)
+            nc.scalar.activation(
+                out=exps[:, cols], in_=picked[:, cols], func=ACT.Exp,
+                bias=neg_max[:, h : h + 1], scale=1.0, accum_out=sums[:, h : h + 1],
+            )
+        neg_m1 = pool.tile([P, 1], F32, name="neg_m1")
+        nc.vector.tensor_tensor(out=neg_m1[:], in0=neg_max[:, 0:1], in1=neg_max[:, 1:2], op=ALU.min)
+        rescale = pool.tile([P, 2], F32, name="rescale")
+        nc.scalar.activation(out=rescale[:], in_=neg_max[:], func=ACT.Exp, bias=neg_m1[:], scale=-1.0)
+        first_sum = pool.tile([P, 1], F32, name="first_sum")
+        nc.vector.tensor_tensor(out=first_sum[:], in0=sums[:, 0:1], in1=rescale[:, 0:1], op=ALU.mult)
+        fine_less_max = pool.tile([P, 1], F32, name="fine_less_max")
+        nc.vector.tensor_tensor(out=fine_less_max[:], in0=fine_col[:], in1=neg_m1[:], op=ALU.add)
+        log_sum = pool.tile([P, 1], F32, name="log_sum")
+        nc.scalar.activation(out=log_sum[:], in_=sums[:, 1:2], func=ACT.Ln, bias=first_sum[:], scale=rescale[:, 1:2])
+
+        dl_first = pool.tile([P, FIRST], F32, name="dl_first")
+        nc.vector.tensor_scalar(
+            out=dl_first[:], in0=picked[:, 0:FIRST], scalar1=log_sum[:], scalar2=fine_less_max[:],
+            op0=ALU.subtract, op1=ALU.add,
+        )
+        up = pool.tile([P, 1], F32, name="up")
+        nc.scalar.activation(out=up[:], in_=log_sum[:], func=ACT.Identity, bias=fine_less_max[:], scale=-1.0)
+        dl_rest = pool.tile([P, I - FIRST], F32, name="dl_rest")
+        nc.scalar.activation(out=dl_rest[:], in_=picked[:, FIRST:I], func=ACT.Identity, bias=up[:], scale=1.0)
+        neg_fine = pool.tile([P, 1], F32, name="neg_fine")
+        nc.scalar.activation(out=neg_fine[:], in_=fine_col[:], func=ACT.Copy, scale=-1.0)
+        nc.vector.tensor_copy(out=placed[:].indirect(offsets[:, 0 : FIRST // 16]), in_=dl_first[:])
+        nc.vector.tensor_copy(out=placed[:].indirect(offsets[:, FIRST // 16 : I // 16]), in_=dl_rest[:])
+
+        for n, (lo, hi) in enumerate(VECTOR_STORES):
+            result = pool.tile([P, hi - lo], F32, name="result%d" % n)
+            nc.vector.tensor_scalar(
+                out=result[:], in0=placed[:, lo:hi], scalar1=fine_col[:], scalar2=None, op0=ALU.subtract
+            )
+            nc.sync.dma_start(out=out[:, lo:hi], in_=result[:])
+        lo, hi = SCALAR_STORE
+        last = pool.tile([P, hi - lo], F32, name="last")
+        nc.scalar.activation(out=last[:], in_=placed[:, lo:hi], func=ACT.Identity, bias=neg_fine[:], scale=1.0)
+        nc.scalar.dma_start(out=out[:, lo:hi], in_=last[:])

@@ -1,3 +1,4 @@
+import math
 from contextlib import ExitStack
 
 import concourse.mybir as mybir
@@ -20,8 +21,13 @@ P = 128
 PACK = 4
 PLANE = 512
 HALF = I // 2
-WORD_LOADS = ((0, 1024), (1024, 1536), (1536, 2048))
-PRODUCTS = ((0, 512), (512, 1024), (1024, 1536), (1536, 1792), (1792, 2048))
+WORD_LOADS = ((0, 512), (512, 1536), (1536, 2048))
+STEPS = 128
+STEP = 7.0 / STEPS
+LINEAR = 20.0 / 27.0
+CONSTANT = 49.0 / 324.0
+ROOT_HALF = math.sqrt(0.5)
+PRODUCTS = ((0, 512), (512, 1024), (1024, 1536), (1536, 1792), (1792, 1920), (1920, 2048))
 FIRST = 256
 VECTOR_STORES = ((0, 256), (256, 768), (768, 1536))
 SCALAR_STORE = (1536, 2048)
@@ -33,27 +39,40 @@ def tile_attend_allowedset_heads_kernel(tc, hid, voc_words, voc_scales, fine, of
         pool = ctx.enter_context(tc.tile_pool(name="pool", bufs=1))
         psum = ctx.enter_context(tc.psum_pool(name="psum", bufs=1))
 
-        offsets = pool.tile([P, I // 16], U16, name="offsets")
         planes = pool.tile([P, PLANE], U8, name="planes", align_bytes=64)
         nc.vector.memset(planes[:].bitcast(I32), 0)
+        hid_raw = pool.tile([P, PACK, Q], F32, name="hid_raw")
+        nc.scalar.dma_start(out=hid_raw[:], in_=hid.rearrange("(p j) q -> p j q", j=PACK))
         for quad in range(4):
             rows = voc_scales[0][4 * quad : 4 * quad + 4, :].bitcast(I32)
-            nc.scalar.dma_start(
+            nc.sync.dma_start(
                 out=planes[32 * quad : 32 * quad + 16, :].bitcast(I32),
                 in_=rows.rearrange("r (c w) -> c r w", c=4),
             )
-
-        hid_raw = pool.tile([P, PACK, Q], F32, name="hid_raw")
-        nc.sync.dma_start(out=hid_raw[:], in_=hid.rearrange("(p j) q -> p j q", j=PACK))
         all_words = voc_words[0].rearrange("p n t -> p (n t)").bitcast(I32)
         words = []
         for n, (lo, hi) in enumerate(WORD_LOADS):
             part = pool.tile([P, hi - lo], U32, name="words%d" % n, align_bytes=64)
             nc.sync.dma_start(out=part[:].bitcast(I32), in_=all_words[:, lo:hi])
             words.append(part)
+        offsets = pool.tile([P, I // 16], U16, name="offsets")
         nc.sync.dma_start(offsets[:], offs)
         fine_col = pool.tile([P, 1], F32, name="fine_col")
         nc.sync.dma_start(out=fine_col[:], in_=fine)
+
+        count_down = pool.tile([P, STEPS], F32, name="count_down")
+        nc.gpsimd.iota(
+            count_down[:], pattern=[[-1, STEPS]], base=STEPS, channel_multiplier=0, allow_small_or_imprecise_dtypes=True
+        )
+        bounds = pool.tile([P, STEPS], F32, name="bounds")
+        nc.scalar.activation(out=bounds[:], in_=count_down[:], func=ACT.Exp, scale=STEP)
+        centres = pool.tile([P, STEPS + 1], F32, name="centres")
+        nc.vector.memset(centres[:, 0:1], 0.0)
+        nc.scalar.activation(out=centres[:, 1:], in_=count_down[:], func=ACT.Exp, scale=-STEP, bias=STEP / 2)
+        rises = pool.tile([P, STEPS], F32, name="rises")
+        nc.vector.tensor_tensor(out=rises[:], in0=centres[:, 1:], in1=centres[:, 0:STEPS], op=ALU.subtract)
+        log_steps = pool.tile([P, STEPS], F32, name="log_steps")
+        nc.vector.memset(log_steps[:, 1:], STEP)
 
         placed = pool.tile([P, V], F32, name="placed")
         nc.vector.memset(placed[:], 0.0)
@@ -97,34 +116,66 @@ def tile_attend_allowedset_heads_kernel(tc, hid, voc_words, voc_scales, fine, of
                 out=picked[:, h * HALF : (h + 1) * HALF],
                 in_=scores[:].indirect(offsets[:, h * HALF // 16 : (h + 1) * HALF // 16]),
             )
-        neg_max = pool.tile([P, 2], F32, name="neg_max")
-        sums = pool.tile([P, 2], F32, name="sums")
+        def column(name):
+            return pool.tile([P, 1], F32, name=name)
+
         exps = pool.tile([P, I], BF16, name="exps")
-        for h in range(2):
-            cols = slice(h * HALF, (h + 1) * HALF)
-            nc.vector.tensor_reduce(out=neg_max[:, h : h + 1], in_=picked[:, cols], axis=AX.X, op=ALU.max, negate=True)
-            nc.scalar.activation(
-                out=exps[:, cols], in_=picked[:, cols], func=ACT.Exp,
-                bias=neg_max[:, h : h + 1], scale=1.0, accum_out=sums[:, h : h + 1],
-            )
-        neg_m1 = pool.tile([P, 1], F32, name="neg_m1")
-        nc.vector.tensor_tensor(out=neg_m1[:], in0=neg_max[:, 0:1], in1=neg_max[:, 1:2], op=ALU.min)
-        rescale = pool.tile([P, 2], F32, name="rescale")
-        nc.scalar.activation(out=rescale[:], in_=neg_max[:], func=ACT.Exp, bias=neg_m1[:], scale=-1.0)
-        first_sum = pool.tile([P, 1], F32, name="first_sum")
-        nc.vector.tensor_tensor(out=first_sum[:], in0=sums[:, 0:1], in1=rescale[:, 0:1], op=ALU.mult)
-        fine_less_max = pool.tile([P, 1], F32, name="fine_less_max")
-        nc.vector.tensor_tensor(out=fine_less_max[:], in0=fine_col[:], in1=neg_m1[:], op=ALU.add)
-        log_sum = pool.tile([P, 1], F32, name="log_sum")
-        nc.scalar.activation(out=log_sum[:], in_=sums[:, 1:2], func=ACT.Ln, bias=first_sum[:], scale=rescale[:, 1:2])
+        neg_max0, neg_max1, neg_m1 = column("neg_max0"), column("neg_max1"), column("neg_m1")
+        sum0, sum1 = column("sum0"), column("sum1")
+        nc.vector.tensor_reduce(out=neg_max0[:], in_=picked[:, 0:HALF], axis=AX.X, op=ALU.max, negate=True)
+        nc.scalar.activation(
+            out=exps[:, 0:HALF], in_=picked[:, 0:HALF], func=ACT.Exp, bias=neg_max0[:], scale=1.0, accum_out=sum0[:]
+        )
+        nc.vector.tensor_reduce(out=neg_max1[:], in_=picked[:, HALF:I], axis=AX.X, op=ALU.max, negate=True)
+        nc.vector.tensor_tensor(out=neg_m1[:], in0=neg_max0[:], in1=neg_max1[:], op=ALU.min)
+        rescale = column("rescale")
+        nc.scalar.activation(out=rescale[:], in_=neg_max0[:], func=ACT.Exp, bias=neg_m1[:], scale=-1.0)
+        nc.scalar.activation(
+            out=exps[:, HALF:I], in_=picked[:, HALF:I], func=ACT.Exp, bias=neg_m1[:], scale=1.0, accum_out=sum1[:]
+        )
+        neg_sum0 = column("neg_sum0")
+        nc.vector.tensor_scalar(out=neg_sum0[:], in0=sum0[:], scalar1=-1.0, scalar2=None, op0=ALU.mult)
+        nc.vector.tensor_scalar(
+            out=log_steps[:, 0:1], in0=fine_col[:], scalar1=neg_m1[:],
+            scalar2=LINEAR - CONSTANT - STEP * (STEPS - 0.5), op0=ALU.add, op1=ALU.add,
+        )
+        bounds1 = pool.tile([P, STEPS], F32, name="bounds1")
+        nc.vector.scalar_tensor_tensor(
+            out=bounds1[:], in0=rescale[:].to_broadcast([P, STEPS]), scalar=neg_sum0[:], in1=bounds[:],
+            op0=ALU.mult, op1=ALU.add,
+        )
+        first_part = column("first_part")
+        nc.vector.tensor_scalar(
+            out=first_part[:], in0=rescale[:], scalar1=sum0[:], scalar2=ROOT_HALF, op0=ALU.mult, op1=ALU.mult
+        )
+        root_sum, linear_sum = column("root_sum"), column("linear_sum")
+        nc.scalar.activation(out=root_sum[:], in_=sum1[:], func=ACT.Identity, bias=first_part[:], scale=ROOT_HALF)
+        nc.scalar.activation(out=linear_sum[:], in_=root_sum[:], func=ACT.Copy, scale=-LINEAR / ROOT_HALF)
+        taken = pool.tile([P, 2, STEPS], F32, name="taken")
+        inverse, coarse = column("inverse"), column("coarse")
+        nc.vector.scalar_tensor_tensor(
+            out=taken[:, 0, :], in0=bounds1[:], scalar=sum1[:], in1=rises[:],
+            op0=ALU.is_gt, op1=ALU.mult, accum_out=inverse[:],
+        )
+        nc.vector.scalar_tensor_tensor(
+            out=taken[:, 1, :], in0=bounds1[:], scalar=sum1[:], in1=log_steps[:],
+            op0=ALU.is_gt, op1=ALU.mult, accum_out=coarse[:],
+        )
+        inner, outer, rest = column("inner"), column("outer"), column("rest")
+        nc.scalar.activation(
+            out=inner[:], in_=inverse[:], func=ACT.Square, scale=root_sum[:], bias=-4.0 / 3.0 * ROOT_HALF
+        )
+        nc.scalar.activation(out=outer[:], in_=inner[:], func=ACT.Square, scale=1.0, bias=1.0 / 3.0)
+        nc.vector.tensor_scalar(
+            out=rest[:], in0=inverse[:], scalar1=linear_sum[:], scalar2=coarse[:], op0=ALU.mult, op1=ALU.add
+        )
 
         dl_first = pool.tile([P, FIRST], F32, name="dl_first")
         nc.vector.tensor_scalar(
-            out=dl_first[:], in0=picked[:, 0:FIRST], scalar1=log_sum[:], scalar2=fine_less_max[:],
-            op0=ALU.subtract, op1=ALU.add,
+            out=dl_first[:], in0=picked[:, 0:FIRST], scalar1=outer[:], scalar2=rest[:], op0=ALU.add, op1=ALU.add
         )
-        up = pool.tile([P, 1], F32, name="up")
-        nc.scalar.activation(out=up[:], in_=log_sum[:], func=ACT.Identity, bias=fine_less_max[:], scale=-1.0)
+        up = column("up")
+        nc.scalar.activation(out=up[:], in_=outer[:], func=ACT.Identity, bias=rest[:], scale=1.0)
         dl_rest = pool.tile([P, I - FIRST], F32, name="dl_rest")
         nc.scalar.activation(out=dl_rest[:], in_=picked[:, FIRST:I], func=ACT.Identity, bias=up[:], scale=1.0)
         neg_fine = pool.tile([P, 1], F32, name="neg_fine")

@@ -21,13 +21,13 @@ P = 128
 PACK = 4
 PLANE = 512
 HALF = I // 2
-WORD_LOADS = ((0, 512), (512, 1536), (1536, 2048))
+WORD_LOADS = ((0, 256), (256, 1024), (1024, 1792), (1792, 2048))
 STEPS = 128
 STEP = 7.0 / STEPS
 LINEAR = 20.0 / 27.0
 CONSTANT = 49.0 / 324.0
 ROOT_HALF = math.sqrt(0.5)
-PRODUCTS = ((0, 512), (512, 1024), (1024, 1536), (1536, 1792), (1792, 1920), (1920, 2048))
+PRODUCTS = ((0, 256), (256, 512), (512, 1024), (1024, 1536), (1536, 1792), (1792, 1920), (1920, 2048))
 FIRST = 256
 VECTOR_STORES = ((0, 256), (256, 768), (768, 1536))
 SCALAR_STORE = (1536, 2048)
@@ -42,7 +42,7 @@ def tile_attend_allowedset_heads_kernel(tc, hid, voc_words, voc_scales, fine, of
         planes = pool.tile([P, PLANE], U8, name="planes", align_bytes=64)
         nc.vector.memset(planes[:].bitcast(I32), 0)
         hid_raw = pool.tile([P, PACK, Q], F32, name="hid_raw")
-        nc.scalar.dma_start(out=hid_raw[:], in_=hid.rearrange("(p j) q -> p j q", j=PACK))
+        nc.sync.dma_start(out=hid_raw[:], in_=hid.rearrange("(p j) q -> p j q", j=PACK))
         for quad in range(4):
             rows = voc_scales[0][4 * quad : 4 * quad + 4, :].bitcast(I32)
             nc.sync.dma_start(
@@ -66,29 +66,35 @@ def tile_attend_allowedset_heads_kernel(tc, hid, voc_words, voc_scales, fine, of
         )
         bounds = pool.tile([P, STEPS], F32, name="bounds")
         nc.scalar.activation(out=bounds[:], in_=count_down[:], func=ACT.Exp, scale=STEP)
-        centres = pool.tile([P, STEPS + 1], F32, name="centres")
-        nc.vector.memset(centres[:, 0:1], 0.0)
-        nc.scalar.activation(out=centres[:, 1:], in_=count_down[:], func=ACT.Exp, scale=-STEP, bias=STEP / 2)
         rises = pool.tile([P, STEPS], F32, name="rises")
-        nc.vector.tensor_tensor(out=rises[:], in0=centres[:, 1:], in1=centres[:, 0:STEPS], op=ALU.subtract)
+        nc.scalar.activation(out=rises[:, 0:1], in_=count_down[:, 0:1], func=ACT.Exp, scale=-STEP, bias=STEP / 2)
+        nc.scalar.activation(
+            out=rises[:, 1:], in_=count_down[:, 1:], func=ACT.Exp, scale=-STEP,
+            bias=STEP / 2 + math.log(1.0 - math.exp(-STEP)),
+        )
         log_steps = pool.tile([P, STEPS], F32, name="log_steps")
         nc.vector.memset(log_steps[:, 1:], STEP)
 
         placed = pool.tile([P, V], F32, name="placed")
         nc.vector.memset(placed[:], 0.0)
 
-        hid_bf = pool.tile([P, Q, PACK], BF16, name="hid_bf", align_bytes=64)
-        nc.vector.tensor_copy(
-            out=hid_bf[:].rearrange("p (c i) t -> p c t i", i=4),
-            in_=hid_raw[:].rearrange("p t (c i) -> p c t i", i=4),
-        )
         hid_codes = pool.tile([P, Q], U32, name="hid_codes", align_bytes=64)
         hid_scales = pool.tile([P, Q], U8, name="hid_scales", align_bytes=64)
-        nc.vector.quantize_mx(
-            out=hid_codes[:].bitcast(FP8X4),
-            scales=hid_scales[:],
-            in_=hid_bf[:].rearrange("p q t -> p (q t)"),
-        )
+        rounded = []
+        for h in range(2):
+            half = pool.tile([P, Q // 2, PACK], BF16, name="hid_bf%d" % h, align_bytes=64)
+            nc.vector.tensor_copy(
+                out=half[:].rearrange("p (c i) t -> p c t i", i=4),
+                in_=hid_raw[:, :, h * Q // 2 : (h + 1) * Q // 2].rearrange("p t (c i) -> p c t i", i=4),
+            )
+            rounded.append(half)
+        for h in range(2):
+            rows = slice(h * Q // 2, (h + 1) * Q // 2)
+            nc.vector.quantize_mx(
+                out=hid_codes[:, rows].bitcast(FP8X4),
+                scales=hid_scales[:, rows],
+                in_=rounded[h][:].rearrange("p q t -> p (q t)"),
+            )
 
         scores = pool.tile([P, V], F32, name="scores")
         for n, (lo, hi) in enumerate(PRODUCTS):

@@ -1,4 +1,3 @@
-import math
 from contextlib import ExitStack
 
 import concourse.mybir as mybir
@@ -22,11 +21,9 @@ PACK = 4
 PLANE = 512
 HALF = I // 2
 WORD_LOADS = ((0, 256), (256, 1024), (1024, 1792), (1792, 2048))
-STEPS = 128
-STEP = 7.0 / STEPS
-LINEAR = 20.0 / 27.0
-CONSTANT = 49.0 / 324.0
-ROOT_HALF = math.sqrt(0.5)
+NODES = 72
+NODES_ABOVE_ONE = 7
+STEP = 7.0 / 16.0
 PRODUCTS = ((0, 256), (256, 512), (512, 1024), (1024, 1536), (1536, 1792), (1792, 1920), (1920, 2048))
 FIRST = 256
 VECTOR_STORES = ((0, 256), (256, 768), (768, 1536))
@@ -60,20 +57,23 @@ def tile_attend_allowedset_heads_kernel(tc, hid, voc_words, voc_scales, fine, of
         fine_col = pool.tile([P, 1], F32, name="fine_col")
         nc.sync.dma_start(out=fine_col[:], in_=fine)
 
-        count_down = pool.tile([P, STEPS], F32, name="count_down")
+        def column(name):
+            return pool.tile([P, 1], F32, name=name)
+
+        count_down = pool.tile([P, NODES], F32, name="count_down")
         nc.gpsimd.iota(
-            count_down[:], pattern=[[-1, STEPS]], base=STEPS, channel_multiplier=0, allow_small_or_imprecise_dtypes=True
+            count_down[:], pattern=[[-1, NODES]], base=NODES_ABOVE_ONE, channel_multiplier=0,
+            allow_small_or_imprecise_dtypes=True,
         )
-        bounds = pool.tile([P, STEPS], F32, name="bounds")
-        nc.scalar.activation(out=bounds[:], in_=count_down[:], func=ACT.Exp, scale=STEP)
-        rises = pool.tile([P, STEPS], F32, name="rises")
-        nc.scalar.activation(out=rises[:, 0:1], in_=count_down[:, 0:1], func=ACT.Exp, scale=-STEP, bias=STEP / 2)
-        nc.scalar.activation(
-            out=rises[:, 1:], in_=count_down[:, 1:], func=ACT.Exp, scale=-STEP,
-            bias=STEP / 2 + math.log(1.0 - math.exp(-STEP)),
-        )
-        log_steps = pool.tile([P, STEPS], F32, name="log_steps")
-        nc.vector.memset(log_steps[:, 1:], STEP)
+        nodes = pool.tile([P, NODES], F32, name="nodes")
+        nc.scalar.activation(out=nodes[:], in_=count_down[:], func=ACT.Exp, scale=STEP)
+        neg_nodes = pool.tile([P, NODES], F32, name="neg_nodes")
+        nc.scalar.activation(out=neg_nodes[:], in_=nodes[:], func=ACT.Copy, scale=-1.0)
+        terms = pool.tile([P, 2, NODES], F32, name="terms")
+        terms_at_one = column("terms_at_one")
+        nc.scalar.activation(out=terms[:, 0, :], in_=neg_nodes[:], func=ACT.Exp, scale=1.0, accum_out=terms_at_one[:])
+        shift = column("shift")
+        nc.scalar.activation(out=shift[:], in_=terms_at_one[:], func=ACT.Copy, scale=-STEP)
 
         placed = pool.tile([P, V], F32, name="placed")
         nc.vector.memset(placed[:], 0.0)
@@ -122,9 +122,6 @@ def tile_attend_allowedset_heads_kernel(tc, hid, voc_words, voc_scales, fine, of
                 out=picked[:, h * HALF : (h + 1) * HALF],
                 in_=scores[:].indirect(offsets[:, h * HALF // 16 : (h + 1) * HALF // 16]),
             )
-        def column(name):
-            return pool.tile([P, 1], F32, name=name)
-
         exps = pool.tile([P, I], BF16, name="exps")
         neg_max0, neg_max1, neg_m1 = column("neg_max0"), column("neg_max1"), column("neg_m1")
         sum0, sum1 = column("sum0"), column("sum1")
@@ -139,53 +136,30 @@ def tile_attend_allowedset_heads_kernel(tc, hid, voc_words, voc_scales, fine, of
         nc.scalar.activation(
             out=exps[:, HALF:I], in_=picked[:, HALF:I], func=ACT.Exp, bias=neg_m1[:], scale=1.0, accum_out=sum1[:]
         )
-        neg_sum0 = column("neg_sum0")
-        nc.vector.tensor_scalar(out=neg_sum0[:], in0=sum0[:], scalar1=-1.0, scalar2=None, op0=ALU.mult)
+        row_sum = column("row_sum")
+        nc.scalar.activation(out=row_sum[:], in_=rescale[:], func=ACT.Identity, bias=sum1[:], scale=sum0[:])
+        known = column("known")
         nc.vector.tensor_scalar(
-            out=log_steps[:, 0:1], in0=fine_col[:], scalar1=neg_m1[:],
-            scalar2=LINEAR - CONSTANT - STEP * (STEPS - 0.5), op0=ALU.add, op1=ALU.add,
+            out=known[:], in0=fine_col[:], scalar1=neg_m1[:], scalar2=shift[:], op0=ALU.add, op1=ALU.add
         )
-        bounds1 = pool.tile([P, STEPS], F32, name="bounds1")
-        nc.vector.scalar_tensor_tensor(
-            out=bounds1[:], in0=rescale[:].to_broadcast([P, STEPS]), scalar=neg_sum0[:], in1=bounds[:],
-            op0=ALU.mult, op1=ALU.add,
-        )
-        first_part = column("first_part")
+        ahead = pool.tile([P, FIRST], F32, name="ahead")
         nc.vector.tensor_scalar(
-            out=first_part[:], in0=rescale[:], scalar1=sum0[:], scalar2=ROOT_HALF, op0=ALU.mult, op1=ALU.mult
+            out=ahead[:], in0=picked[:, 0:FIRST], scalar1=known[:], scalar2=1.0 / STEP, op0=ALU.add, op1=ALU.mult
         )
-        root_sum, linear_sum = column("root_sum"), column("linear_sum")
-        nc.scalar.activation(out=root_sum[:], in_=sum1[:], func=ACT.Identity, bias=first_part[:], scale=ROOT_HALF)
-        nc.scalar.activation(out=linear_sum[:], in_=root_sum[:], func=ACT.Copy, scale=-LINEAR / ROOT_HALF)
-        taken = pool.tile([P, 2, STEPS], F32, name="taken")
-        inverse, coarse = column("inverse"), column("coarse")
-        nc.vector.scalar_tensor_tensor(
-            out=taken[:, 0, :], in0=bounds1[:], scalar=sum1[:], in1=rises[:],
-            op0=ALU.is_gt, op1=ALU.mult, accum_out=inverse[:],
-        )
-        nc.vector.scalar_tensor_tensor(
-            out=taken[:, 1, :], in0=bounds1[:], scalar=sum1[:], in1=log_steps[:],
-            op0=ALU.is_gt, op1=ALU.mult, accum_out=coarse[:],
-        )
-        inner, outer, rest = column("inner"), column("outer"), column("rest")
+        terms_at_sum = column("terms_at_sum")
         nc.scalar.activation(
-            out=inner[:], in_=inverse[:], func=ACT.Square, scale=root_sum[:], bias=-4.0 / 3.0 * ROOT_HALF
+            out=terms[:, 1, :], in_=neg_nodes[:], func=ACT.Exp, scale=row_sum[:], accum_out=terms_at_sum[:]
         )
-        nc.scalar.activation(out=outer[:], in_=inner[:], func=ACT.Square, scale=1.0, bias=1.0 / 3.0)
-        nc.vector.tensor_scalar(
-            out=rest[:], in0=inverse[:], scalar1=linear_sum[:], scalar2=coarse[:], op0=ALU.mult, op1=ALU.add
-        )
-
         dl_first = pool.tile([P, FIRST], F32, name="dl_first")
         nc.vector.tensor_scalar(
-            out=dl_first[:], in0=picked[:, 0:FIRST], scalar1=outer[:], scalar2=rest[:], op0=ALU.add, op1=ALU.add
+            out=dl_first[:], in0=ahead[:], scalar1=terms_at_sum[:], scalar2=STEP, op0=ALU.add, op1=ALU.mult
         )
         up = column("up")
-        nc.scalar.activation(out=up[:], in_=outer[:], func=ACT.Identity, bias=rest[:], scale=1.0)
+        nc.scalar.activation(out=up[:], in_=terms_at_sum[:], func=ACT.Identity, bias=known[:], scale=STEP)
         dl_rest = pool.tile([P, I - FIRST], F32, name="dl_rest")
         nc.scalar.activation(out=dl_rest[:], in_=picked[:, FIRST:I], func=ACT.Identity, bias=up[:], scale=1.0)
         neg_fine = pool.tile([P, 1], F32, name="neg_fine")
-        nc.scalar.activation(out=neg_fine[:], in_=fine_col[:], func=ACT.Copy, scale=-1.0)
+        nc.gpsimd.tensor_scalar(out=neg_fine[:], in0=fine_col[:], scalar1=-1.0, scalar2=0.0, op0=ALU.mult, op1=ALU.add)
         nc.vector.tensor_copy(out=placed[:].indirect(offsets[:, 0 : FIRST // 16]), in_=dl_first[:])
         nc.vector.tensor_copy(out=placed[:].indirect(offsets[:, FIRST // 16 : I // 16]), in_=dl_rest[:])
 

@@ -20,11 +20,11 @@ P = 128
 PACK = 4
 PLANE = 512
 HALF = I // 2
-WORD_LOADS = ((0, 256), (256, 1024), (1024, 1792), (1792, 2048))
+WORD_LOADS = ((0, 256), (256, 768), (768, 1280), (1280, 1792), (1792, 2048))
 NODES = 72
 NODES_ABOVE_ONE = 7
 STEP = 7.0 / 16.0
-PRODUCTS = ((0, 256), (256, 512), (512, 1024), (1024, 1536), (1536, 1792), (1792, 1920), (1920, 2048))
+PRODUCTS = tuple((lo, lo + 256) for lo in range(0, 1792, 256)) + ((1792, 1920), (1920, 2048))
 FIRST = 256
 VECTOR_STORES = ((0, 256), (256, 768), (768, 1536))
 SCALAR_STORE = (1536, 2048)
@@ -101,7 +101,7 @@ def tile_attend_allowedset_heads_kernel(tc, hid, voc_words, voc_scales, fine, of
             load = max(k for k, (start, end) in enumerate(WORD_LOADS) if start <= lo)
             base = WORD_LOADS[load][0]
             c = lo // PLANE
-            bank = psum.tile([P, hi - lo], F32, name="bank%d" % n)
+            bank = psum.tile([P, hi - lo], F32, name="bank%d" % (n % 8))
             nc.tensor.matmul_mx(
                 out=bank[:],
                 lhsT=hid_codes[:].bitcast(FP8X4),

from contextlib import ExitStack

import concourse.mybir as mybir

D, V, Q, I = 512, 2048, 128, 1024
FLOPS = 2 * D * V * Q

F32 = mybir.dt.float32
BF16 = mybir.dt.bfloat16
I32 = mybir.dt.int32
U32 = mybir.dt.uint32
U16 = mybir.dt.uint16
U8 = mybir.dt.uint8
FP8X4 = mybir.dt.float8_e4m3fn_x4
ALU = mybir.AluOpType
ACT = mybir.ActivationFunctionType
AX = mybir.AxisListType

P = 128
PACK = 4
PLANE = 512
HALF = I // 2
WORD_LOADS = ((0, 256), (256, 768), (768, 1280), (1280, 1792), (1792, 2048))
NODES = 72
NODES_ABOVE_ONE = 7
STEP = 7.0 / 16.0
PRODUCTS = tuple((lo, lo + 256) for lo in range(0, 1792, 256)) + ((1792, 1920), (1920, 2048))
FIRST = 256
VECTOR_STORES = ((0, 256), (256, 768), (768, 1536))
SCALAR_STORE = (1536, 2048)


def tile_attend_allowedset_heads_kernel(tc, hid, voc_words, voc_scales, fine, offs, out):
    nc = tc.nc
    with ExitStack() as ctx:
        pool = ctx.enter_context(tc.tile_pool(name="pool", bufs=1))
        psum = ctx.enter_context(tc.psum_pool(name="psum", bufs=1))

        planes = pool.tile([P, PLANE], U8, name="planes", align_bytes=64)
        nc.vector.memset(planes[:].bitcast(I32), 0)
        hid_raw = pool.tile([P, PACK, Q], F32, name="hid_raw")
        nc.sync.dma_start(out=hid_raw[:], in_=hid.rearrange("(p j) q -> p j q", j=PACK))
        for quad in range(4):
            rows = voc_scales[0][4 * quad : 4 * quad + 4, :].bitcast(I32)
            nc.sync.dma_start(
                out=planes[32 * quad : 32 * quad + 16, :].bitcast(I32),
                in_=rows.rearrange("r (c w) -> c r w", c=4),
            )
        all_words = voc_words[0].rearrange("p n t -> p (n t)").bitcast(I32)
        words = []
        for n, (lo, hi) in enumerate(WORD_LOADS):
            part = pool.tile([P, hi - lo], U32, name="words%d" % n, align_bytes=64)
            nc.sync.dma_start(out=part[:].bitcast(I32), in_=all_words[:, lo:hi])
            words.append(part)
        offsets = pool.tile([P, I // 16], U16, name="offsets")
        nc.sync.dma_start(offsets[:], offs)
        fine_col = pool.tile([P, 1], F32, name="fine_col")
        nc.sync.dma_start(out=fine_col[:], in_=fine)

        def column(name):
            return pool.tile([P, 1], F32, name=name)

        count_down = pool.tile([P, NODES], F32, name="count_down")
        nc.gpsimd.iota(
            count_down[:], pattern=[[-1, NODES]], base=NODES_ABOVE_ONE, channel_multiplier=0,
            allow_small_or_imprecise_dtypes=True,
        )
        nodes = pool.tile([P, NODES], F32, name="nodes")
        nc.scalar.activation(out=nodes[:], in_=count_down[:], func=ACT.Exp, scale=STEP)
        neg_nodes = pool.tile([P, NODES], F32, name="neg_nodes")
        nc.scalar.activation(out=neg_nodes[:], in_=nodes[:], func=ACT.Copy, scale=-1.0)
        terms = pool.tile([P, 2, NODES], F32, name="terms")
        terms_at_one = column("terms_at_one")
        nc.scalar.activation(out=terms[:, 0, :], in_=neg_nodes[:], func=ACT.Exp, scale=1.0, accum_out=terms_at_one[:])
        shift = column("shift")
        nc.scalar.activation(out=shift[:], in_=terms_at_one[:], func=ACT.Copy, scale=-STEP)

        placed = pool.tile([P, V], F32, name="placed")
        nc.vector.memset(placed[:], 0.0)

        hid_codes = pool.tile([P, Q], U32, name="hid_codes", align_bytes=64)
        hid_scales = pool.tile([P, Q], U8, name="hid_scales", align_bytes=64)
        rounded = []
        for h in range(2):
            half = pool.tile([P, Q // 2, PACK], BF16, name="hid_bf%d" % h, align_bytes=64)
            nc.vector.tensor_copy(
                out=half[:].rearrange("p (c i) t -> p c t i", i=4),
                in_=hid_raw[:, :, h * Q // 2 : (h + 1) * Q // 2].rearrange("p t (c i) -> p c t i", i=4),
            )
            rounded.append(half)
        for h in range(2):
            rows = slice(h * Q // 2, (h + 1) * Q // 2)
            nc.vector.quantize_mx(
                out=hid_codes[:, rows].bitcast(FP8X4),
                scales=hid_scales[:, rows],
                in_=rounded[h][:].rearrange("p q t -> p (q t)"),
            )

        scores = pool.tile([P, V], F32, name="scores")
        for n, (lo, hi) in enumerate(PRODUCTS):
            load = max(k for k, (start, end) in enumerate(WORD_LOADS) if start <= lo)
            base = WORD_LOADS[load][0]
            c = lo // PLANE
            bank = psum.tile([P, hi - lo], F32, name="bank%d" % (n % 8))
            nc.tensor.matmul_mx(
                out=bank[:],
                lhsT=hid_codes[:].bitcast(FP8X4),
                lhsT_scale=hid_scales[:],
                rhs=words[load][:, lo - base : hi - base].bitcast(FP8X4),
                rhs_scale=planes[4 * c : P, lo - c * PLANE : hi - c * PLANE],
                start=True,
                stop=True,
            )
            if n % 2 == 0:
                nc.scalar.copy(out=scores[:, lo:hi], in_=bank[:])
            else:
                nc.vector.tensor_copy(out=scores[:, lo:hi], in_=bank[:])

        picked = pool.tile([P, I], F32, name="picked")
        for h in range(2):
            nc.vector.tensor_copy(
                out=picked[:, h * HALF : (h + 1) * HALF],
                in_=scores[:].indirect(offsets[:, h * HALF // 16 : (h + 1) * HALF // 16]),
            )
        exps = pool.tile([P, I], BF16, name="exps")
        neg_max0, neg_max1, neg_m1 = column("neg_max0"), column("neg_max1"), column("neg_m1")
        sum0, sum1 = column("sum0"), column("sum1")
        nc.vector.tensor_reduce(out=neg_max0[:], in_=picked[:, 0:HALF], axis=AX.X, op=ALU.max, negate=True)
        nc.scalar.activation(
            out=exps[:, 0:HALF], in_=picked[:, 0:HALF], func=ACT.Exp, bias=neg_max0[:], scale=1.0, accum_out=sum0[:]
        )
        nc.vector.tensor_reduce(out=neg_max1[:], in_=picked[:, HALF:I], axis=AX.X, op=ALU.max, negate=True)
        nc.vector.tensor_tensor(out=neg_m1[:], in0=neg_max0[:], in1=neg_max1[:], op=ALU.min)
        rescale = column("rescale")
        nc.scalar.activation(out=rescale[:], in_=neg_max0[:], func=ACT.Exp, bias=neg_m1[:], scale=-1.0)
        nc.scalar.activation(
            out=exps[:, HALF:I], in_=picked[:, HALF:I], func=ACT.Exp, bias=neg_m1[:], scale=1.0, accum_out=sum1[:]
        )
        row_sum = column("row_sum")
        nc.scalar.activation(out=row_sum[:], in_=rescale[:], func=ACT.Identity, bias=sum1[:], scale=sum0[:])
        known = column("known")
        nc.vector.tensor_scalar(
            out=known[:], in0=fine_col[:], scalar1=neg_m1[:], scalar2=shift[:], op0=ALU.add, op1=ALU.add
        )
        ahead = pool.tile([P, FIRST], F32, name="ahead")
        nc.vector.tensor_scalar(
            out=ahead[:], in0=picked[:, 0:FIRST], scalar1=known[:], scalar2=1.0 / STEP, op0=ALU.add, op1=ALU.mult
        )
        terms_at_sum = column("terms_at_sum")
        nc.scalar.activation(
            out=terms[:, 1, :], in_=neg_nodes[:], func=ACT.Exp, scale=row_sum[:], accum_out=terms_at_sum[:]
        )
        dl_first = pool.tile([P, FIRST], F32, name="dl_first")
        nc.vector.tensor_scalar(
            out=dl_first[:], in0=ahead[:], scalar1=terms_at_sum[:], scalar2=STEP, op0=ALU.add, op1=ALU.mult
        )
        up = column("up")
        nc.scalar.activation(out=up[:], in_=terms_at_sum[:], func=ACT.Identity, bias=known[:], scale=STEP)
        dl_rest = pool.tile([P, I - FIRST], F32, name="dl_rest")
        nc.scalar.activation(out=dl_rest[:], in_=picked[:, FIRST:I], func=ACT.Identity, bias=up[:], scale=1.0)
        neg_fine = pool.tile([P, 1], F32, name="neg_fine")
        nc.gpsimd.tensor_scalar(out=neg_fine[:], in0=fine_col[:], scalar1=-1.0, scalar2=0.0, op0=ALU.mult, op1=ALU.add)
        nc.vector.tensor_copy(out=placed[:].indirect(offsets[:, 0 : FIRST // 16]), in_=dl_first[:])
        nc.vector.tensor_copy(out=placed[:].indirect(offsets[:, FIRST // 16 : I // 16]), in_=dl_rest[:])

        for n, (lo, hi) in enumerate(VECTOR_STORES):
            result = pool.tile([P, hi - lo], F32, name="result%d" % n)
            nc.vector.tensor_scalar(
                out=result[:], in0=placed[:, lo:hi], scalar1=fine_col[:], scalar2=None, op0=ALU.subtract
            )
            nc.sync.dma_start(out=out[:, lo:hi], in_=result[:])
        lo, hi = SCALAR_STORE
        last = pool.tile([P, hi - lo], F32, name="last")
        nc.scalar.activation(out=last[:], in_=placed[:, lo:hi], func=ACT.Identity, bias=neg_fine[:], scale=1.0)
        nc.scalar.dma_start(out=out[:, lo:hi], in_=last[:])
